import numpy as np
import ml_dtypes


def mxq(x, axis, fmt="e4m3"):
    dtype, down = {"e4m3": (ml_dtypes.float8_e4m3fn, 7), "e5m2": (ml_dtypes.float8_e5m2, 14)}[fmt]
    v = np.moveaxis(np.asarray(x, np.float32).astype(ml_dtypes.bfloat16).astype(np.float64), axis, -1)
    blocks = v.reshape(v.shape[:-1] + (-1, 32))
    amax = np.abs(blocks).max(-1, keepdims=True)
    byte = np.maximum(np.where(amax > 0, np.frexp(amax)[1] - 1 + 127, 0) - down, 1)
    scale = np.exp2(byte - 127.0)
    codes = (blocks / scale).astype(np.float32).astype(dtype).astype(np.float64)
    return np.moveaxis((codes * scale).reshape(v.shape), -1, axis)


WIDE = False


def mx_kscale(k):
    if not WIDE:
        return np.ones(k)
    levels = np.array([10, -10, 5, -5, 0])
    if k % 512:
        return np.exp2(np.random.permutation(np.resize(levels, k // 32))).repeat(32)
    a = np.empty((k // 512, 16))
    for p in range(k // 512):
        a[p, :8] = np.random.permutation(np.resize(levels, 8))
        for g in range(8):
            far = levels[np.abs(levels - a[p, g]) >= 10]
            a[p, g + 8] = far[np.random.randint(len(far))]
    return np.exp2(a.ravel()).repeat(32)


def f64(x):
    return np.asarray(x).astype(np.float64)


def striped(idx):
    return np.tile(np.asarray(idx).reshape(-1, 16).T, (8, 1)).astype(np.uint16)


def unstriped(offs):
    return offs[:16].T.reshape(-1).astype(np.int64)


E2M1 = np.array([0.0, 0.5, 1.0, 1.5, 2.0, 3.0, 4.0, 6.0, -0.0, -0.5, -1.0, -1.5, -2.0, -3.0, -4.0, -6.0])


def pack_weight(w, fmt):
    k, n = w.shape
    w = f64(np.asarray(w, np.float32).astype(ml_dtypes.bfloat16)).reshape(k // 32, 32, n)
    amax = np.abs(w).max(1)
    if fmt == "e4m3":
        byte = np.frexp(amax)[1] - 1 + 127 - 7
    else:
        mant, ex = np.frexp(amax / 6.0)
        byte = np.where(mant > 0.5, ex, ex - 1) + 127
    byte = np.clip(np.where(amax > 0, byte, 1), 1, 254)
    scaled = (w * np.exp2(127.0 - byte)[:, None, :]).reshape(k, n).astype(np.float32)
    by_word = np.ascontiguousarray(scaled.reshape(k // 512, 128, 4, n).transpose(0, 1, 3, 2))
    if fmt == "e4m3":
        words = by_word.astype(ml_dtypes.float8_e4m3fn).view(np.uint8)
    else:
        c = by_word.astype(ml_dtypes.float4_e2m1fn).view(np.uint8) & 0xF
        words = (c[..., 0::2] | (c[..., 1::2] << 4)).reshape(k // 512, 128, 2 * n)
    return np.ascontiguousarray(words), np.ascontiguousarray(byte.astype(np.uint8).reshape(k // 512, 16, n))


def unpack_weight(words, scales, fmt):
    g, _, n = scales.shape
    words = np.ascontiguousarray(words).reshape(g, 128, n, -1)
    if fmt == "e4m3":
        vals = words.view(ml_dtypes.float8_e4m3fn).astype(np.float64)
    else:
        nib = np.empty((g, 128, n, 4), np.uint8)
        nib[..., 0::2] = words & 0xF
        nib[..., 1::2] = words >> 4
        vals = E2M1[nib]
    vals = vals * np.repeat(np.exp2(scales.astype(np.float64) - 127.0), 8, axis=1)[..., None]
    return vals.transpose(0, 1, 3, 2).reshape(g * 512, n)


def bf(x):
    return np.asarray(x, np.float32).astype(ml_dtypes.bfloat16)


def planes(Y):
    r, m = Y.shape
    b = f64(bf(Y)).reshape(r // 32, 32, m)
    amax = np.abs(b).max(1)
    byte = np.clip(np.where(amax > 0, np.frexp(amax)[1] - 1 + 127 - 7, 1), 1, 254)
    codes = (b * np.exp2(127.0 - byte)[:, None, :]).reshape(r, m).astype(np.float32).astype(ml_dtypes.float8_e4m3fn).view(np.uint8)
    words = codes.reshape(r // 512, 128, 4, m).transpose(0, 1, 3, 2)
    return np.ascontiguousarray(words), np.ascontiguousarray(byte.astype(np.uint8).reshape(r // 512, 16, m))


D, T, I, J, U, Z, E, M = 512, 2048, 512, 512, 1024, 1024, 512, 1024


def setup_inputs():
    n = np.random.standard_normal
    idx = np.random.permutation(T)[:I]
    idx2 = np.random.permutation(U)[:J]
    idx3 = np.random.permutation(Z)[:J]
    idx4 = np.random.permutation(M)[:J]
    fd = mx_kscale(D)
    fi = mx_kscale(I)
    ti = np.ones(T)
    ti[idx] = fi
    keysp = pack_weight(n((D, T)) / fd[:, None], "e2m1")
    return {
        "keys_words": keysp[0],
        "keys_scales": keysp[1],
        "notes": (n((D, U)) * 1.0 / np.sqrt(D) * fd[:, None]).astype(np.float32),
        "users2": (n((D, Z)) * 1.0 / np.sqrt(D) * fd[:, None]).astype(np.float32),
        "rowf": (np.random.uniform(0.02, 0.08, (I, 1)) * fi[:, None]).astype(np.float32),
        "vals": (n((E, T)) / ti).astype(np.float32),
        "old": (1.0 * n((E, M))).astype(np.float32),
        "offs": striped(idx),
        "offs2": striped(idx2),
        "offs3": striped(idx3),
        "offs4": striped(idx4),
    }


def reference(keys_words, keys_scales, notes, users2, rowf, vals, old, offs, offs2, offs3, offs4):
    idx = unstriped(offs)
    idx2 = unstriped(offs2)
    idx3 = unstriped(offs3)
    idx4 = unstriped(offs4)
    keysu = unpack_weight(keys_words, keys_scales, "e2m1")
    keysidxg = keysu[:, idx]
    notesq = mxq(f64(notes), 0, "e4m3")
    g1 = keysidxg.T @ notesq
    users2idx3q = mxq(f64(users2)[:, idx3], 0, "e4m3")
    g2 = keysidxg.T @ users2idx3q
    g0 = np.maximum(g1[:, idx2], g2)
    gr1 = g0 * f64(rowf)
    vt1 = f64(vals)[:, idx].T
    vt1q = mxq(vt1, 0, "e4m3")
    gr1q = mxq(gr1, 0, "e4m3")
    o = vt1q.T @ gr1q
    of = np.zeros((E, M))
    of[:, idx4] = o
    y = f64(old) + of
    words, scales = planes(y)
    return y, words, scales

@@ -1,0 +1,210 @@
+from contextlib import ExitStack
+
+import concourse.mybir as mybir
+from concourse.masks import make_identity
+
+D, T, I, J, U, Z, E, M = 512, 2048, 512, 512, 1024, 1024, 512, 1024
+FLOPS = 2 * D * I * U + 2 * D * I * J + 2 * I * E * J
+
+F32 = mybir.dt.float32
+BF16 = mybir.dt.bfloat16
+I32 = mybir.dt.int32
+U32 = mybir.dt.uint32
+U16 = mybir.dt.uint16
+U8 = mybir.dt.uint8
+FP8X4 = mybir.dt.float8_e4m3fn_x4
+FP4X4 = mybir.dt.float4_e2m1fn_x4
+COPY = mybir.ActivationFunctionType.Copy
+ALU = mybir.AluOpType
+
+P = 128
+PACK = 4
+BANK = 512
+PER_COLUMN = 16
+HALF = 256
+SPLIT = 320
+
+
+def interleaved(tile3):
+    return tile3.rearrange("p (c x) t -> p c t x", x=4)
+
+
+def planar(tile3):
+    return tile3.rearrange("p t (c x) -> p c t x", x=4)
+
+
+def quantise(nc, codes, scales, grouped):
+    nc.vector.quantize_mx(out=codes.bitcast(FP8X4), scales=scales, in_=grouped.rearrange("p n t -> p (n t)"))
+
+
+def move(nc, on_vector, out, in_):
+    if on_vector:
+        nc.vector.tensor_copy(out, in_)
+    else:
+        nc.scalar.activation(out, in_, COPY)
+
+
+def tile_attend_tab_wideandown_put_pl_kernel(
+    tc, keys_words, keys_scales, notes, users2, rowf, vals, old, offs, offs2, offs3, offs4, out_0, out_1, out_2
+):
+    nc = tc.nc
+    with ExitStack() as ctx:
+        sb = ctx.enter_context(tc.tile_pool(name="sb", bufs=1))
+        ps = ctx.enter_context(tc.psum_pool(name="ps", bufs=1))
+
+        def tile(shape, dtype, name):
+            return sb.tile(shape, dtype, name=name, align_bytes=64)
+
+        def load_list(source, name):
+            held = sb.tile([P, I // PER_COLUMN], U16, name=name)
+            nc.sync.dma_start(held[:], source)
+            return held
+
+        def load_plane(source, t, name):
+            width = source.shape[1]
+            held = tile([P, width], F32, name)
+            nc.sync.dma_start(held[:], source.rearrange("(p t) n -> t p n", t=PACK)[t])
+            return held
+
+        key_scale_rows = tile([P, T], U8, "key_scale_rows")
+        for q in range(4):
+            nc.sync.dma_start(
+                key_scale_rows[32 * q : 32 * q + 4, :].bitcast(I32),
+                keys_scales[0, 4 * q : 4 * q + 4, :].bitcast(I32),
+            )
+        token_list = load_list(offs, "token_list")
+        key_word_pool = tile([P, T], U16, "key_word_pool")
+        nc.sync.dma_start(key_word_pool[:].bitcast(I32), keys_words[0].bitcast(I32))
+        notes_by_place = notes.rearrange("(p t) u -> p t u", t=PACK)
+        notes_raw = []
+        for h in range(U // HALF):
+            raw = tile([P, PACK, HALF], F32, f"notes_raw{h}")
+            nc.sync.dma_start(raw[:], notes_by_place[:, :, h * HALF : (h + 1) * HALF])
+            notes_raw.append(raw)
+        user_list = load_list(offs3, "user_list")
+        users = [load_plane(users2, t, f"users{t}") for t in range(PACK)]
+        note_list = load_list(offs2, "note_list")
+        row_factor = tile([P, PACK], F32, "row_factor")
+        nc.sync.dma_start(row_factor[:], rowf.rearrange("(s r) one -> s (r one)", r=PACK))
+        place_list = load_list(offs4, "place_list")
+        values = [load_plane(vals, t, f"values{t}") for t in range(PACK)]
+        before = [load_plane(old, t, f"before{t}") for t in range(PACK)]
+
+        key_scale_pool = tile([P, T], U8, "key_scale_pool")
+        nc.vector.memset(key_scale_pool[:].bitcast(I32), 0)
+        for q in range(4):
+            rows = slice(32 * q, 32 * q + 4)
+            nc.vector.tensor_copy(key_scale_pool[rows, :].bitcast(I32), key_scale_rows[rows, :].bitcast(I32))
+
+        def bank_tile(shape, number):
+            return ps.tile(shape, F32, name=f"bank{number}")
+
+        identity = tile([P, P], F32, "identity")
+        make_identity(nc, identity[:])
+        placed = []
+        for t in range(PACK):
+            window = tile([P, M], F32, f"placed{t}")
+            nc.vector.memset(window[:], 0.0)
+            placed.append(window)
+
+        key_words_listed = tile([P, I], U16, "key_words_listed")
+        nc.vector.tensor_copy(key_words_listed[:], key_word_pool[:].indirect(token_list[:]))
+        key_words = tile([P, PACK, P], U16, "key_words")
+        nc.vector.tensor_copy(key_words[:], key_words_listed[:].rearrange("p (s r) -> p r s", r=PACK))
+        key_scales = tile([P, PACK, P], U8, "key_scales")
+        nc.vector.tensor_copy(key_scales[:].rearrange("p r s -> p s r"), key_scale_pool[:].indirect(token_list[:]))
+
+        def key_product(bank, r, codes, scales):
+            nc.tensor.matmul_mx(
+                out=bank, lhsT=key_words[:, r, :].bitcast(FP4X4), lhsT_scale=key_scales[:, r, :],
+                rhs=codes.bitcast(FP8X4), rhs_scale=scales, start=True, stop=True,
+            )
+
+        wide = [tile([P, U], F32, f"wide{r}") for r in range(PACK)]
+        for h in range(U // HALF):
+            grouped = tile([P, HALF, PACK], BF16, f"notes_grouped{h}")
+            move(nc, h >= 2, interleaved(grouped[:]), planar(notes_raw[h][:]))
+            codes = tile([P, HALF], U32, f"notes_codes{h}")
+            scales = tile([P, HALF], U8, f"notes_scales{h}")
+            quantise(nc, codes[:], scales[:], grouped[:])
+            for r in range(PACK):
+                bank = bank_tile([P, HALF], r)
+                key_product(bank[:], r, codes[:], scales[:])
+                nc.scalar.activation(wide[r][:, h * HALF : (h + 1) * HALF], bank[:], COPY)
+
+        users_listed = tile([P, PACK, J], BF16, "users_listed")
+        for t in range(PACK):
+            move(nc, True, users_listed[:, t, :], users[t][:].indirect(user_list[:]))
+        users_grouped = tile([P, J, PACK], BF16, "users_grouped")
+        nc.vector.tensor_copy(interleaved(users_grouped[:]), planar(users_listed[:]))
+        users_codes = tile([P, J], U32, "users_codes")
+        users_scales = tile([P, J], U8, "users_scales")
+        quantise(nc, users_codes[:], users_scales[:], users_grouped[:])
+
+        table = tile([P, PACK, J], F32, "table")
+        for r in range(PACK):
+            wide_listed = tile([P, J], F32, f"wide_listed{r}")
+            nc.scalar.activation(wide_listed[:], wide[r][:].indirect(note_list[:]), COPY)
+            bank = bank_tile([P, J], PACK + r)
+            key_product(bank[:], r, users_codes[:], users_scales[:])
+            nc.vector.tensor_tensor(table[:, r, :], bank[:], wide_listed[:], ALU.max)
+        table_grouped = tile([P, J, PACK], BF16, "table_grouped")
+        factor = row_factor[:].rearrange("p (a r b) -> p a r b", a=1, b=1).to_broadcast([P, J // 4, PACK, 4])
+        nc.vector.tensor_tensor(interleaved(table_grouped[:]), planar(table[:]), factor, ALU.mult)
+        table_codes = tile([P, J], U32, "table_codes")
+        table_scales = tile([P, J], U8, "table_scales")
+        quantise(nc, table_codes[:], table_scales[:], table_grouped[:])
+
+        value_codes = []
+        value_scales = []
+        for t in range(PACK):
+            listed = tile([P, I], BF16, f"values_listed{t}")
+            nc.scalar.activation(listed[:], values[t][:].indirect(token_list[:]), COPY)
+            pairs = listed[:].bitcast(F32)
+            bank = bank_tile([P, 2, P], t % 2)
+            for u in range(2):
+                nc.tensor.transpose(bank[:, u, :], pairs[:, u : I // 2 : 2], identity[:])
+            grouped = tile([P, P, PACK], BF16, f"values_grouped{t}")
+            nc.scalar.copy(grouped[:].bitcast(F32), bank[:].rearrange("s u p -> s p u"))
+            codes = tile([P, P], U32, f"values_codes{t}")
+            scales = tile([P, P], U8, f"values_scales{t}")
+            quantise(nc, codes[:], scales[:], grouped[:])
+            value_codes.append(codes)
+            value_scales.append(scales)
+
+        for t in range(PACK):
+            bank = bank_tile([P, J], (2, 1, 1, 3)[t])
+            nc.tensor.matmul_mx(
+                out=bank[:], lhsT=value_codes[t][:].bitcast(FP8X4), lhsT_scale=value_scales[t][:],
+                rhs=table_codes[:].bitcast(FP8X4), rhs_scale=table_scales[:], start=True, stop=True,
+            )
+            product = tile([P, J], F32, f"product{t}")
+            move(nc, t in (0, 3), product[:], bank[:])
+            cuts = ((0, J), (0, HALF, J), (0, HALF, J), (0, SPLIT, J))[t]
+            for a, b in zip(cuts, cuts[1:]):
+                on_vector = t == 0 or (t == 3 and a == 0)
+                part = place_list[:, a // PER_COLUMN : b // PER_COLUMN]
+                move(nc, on_vector, placed[t][:].indirect(part), product[:, a:b])
+
+        result_grouped = [tile([P, BANK, PACK], BF16, f"result_grouped{h}") for h in range(M // BANK)]
+        out_planes = out_0.rearrange("(p t) m -> t p m", t=PACK)
+        for pair in range(2):
+            result = tile([P, 2, M], F32, f"result{pair}")
+            for half in range(2):
+                t = 2 * pair + half
+                nc.vector.tensor_tensor(result[:, half, :], before[t][:], placed[t][:], ALU.add)
+                nc.sync.dma_start(out_planes[t], result[:, half, :])
+            for h in range(M // BANK):
+                cols = slice(h * BANK, (h + 1) * BANK)
+                move(nc, h == 0, interleaved(result_grouped[h][:, :, 2 * pair : 2 * pair + 2]), planar(result[:, :, cols]))
+        result_codes = tile([P, M], U32, "result_codes")
+        result_scales = tile([P, M], U8, "result_scales")
+        words_out = out_1[0].rearrange("p m t -> p (m t)").bitcast(I32)
+        for h in range(M // BANK):
+            cols = slice(h * BANK, (h + 1) * BANK)
+            quantise(nc, result_codes[:, cols], result_scales[:, cols], result_grouped[h][:])
+            nc.sync.dma_start(words_out[:, cols], result_codes[:, cols].bitcast(I32))
+        for q in range(4):
+            nc.scalar.dma_start(
+                out_2[0, 4 * q : 4 * q + 4, :].bitcast(I32), result_scales[32 * q : 32 * q + 4, :].bitcast(I32)
+            )

@@ -22,7 +22,7 @@ PACK = 4
 BANK = 512
 PER_COLUMN = 16
 HALF = 256
-SPLIT = 320
+SPLIT = 128
 
 
 def interleaved(tile3):
@@ -52,8 +52,8 @@ def tile_attend_tab_wideandown_put_pl_kernel(
         sb = ctx.enter_context(tc.tile_pool(name="sb", bufs=1))
         ps = ctx.enter_context(tc.psum_pool(name="ps", bufs=1))
 
-        def tile(shape, dtype, name):
-            return sb.tile(shape, dtype, name=name, align_bytes=64)
+        def tile(shape, dtype, name, tag=""):
+            return sb.tile(shape, dtype, name=name, tag=tag, align_bytes=64)
 
         def load_list(source, name):
             held = sb.tile([P, I // PER_COLUMN], U16, name=name)
@@ -66,13 +66,13 @@ def tile_attend_tab_wideandown_put_pl_kernel(
             nc.sync.dma_start(held[:], source.rearrange("(p t) n -> t p n", t=PACK)[t])
             return held
 
+        token_list = load_list(offs, "token_list")
         key_scale_rows = tile([P, T], U8, "key_scale_rows")
         for q in range(4):
-            nc.sync.dma_start(
+            nc.scalar.dma_start(
                 key_scale_rows[32 * q : 32 * q + 4, :].bitcast(I32),
                 keys_scales[0, 4 * q : 4 * q + 4, :].bitcast(I32),
             )
-        token_list = load_list(offs, "token_list")
         key_word_pool = tile([P, T], U16, "key_word_pool")
         nc.sync.dma_start(key_word_pool[:].bitcast(I32), keys_words[0].bitcast(I32))
         notes_by_place = notes.rearrange("(p t) u -> p t u", t=PACK)
@@ -91,7 +91,7 @@ def tile_attend_tab_wideandown_put_pl_kernel(
         before = [load_plane(old, t, f"before{t}") for t in range(PACK)]
 
         key_scale_pool = tile([P, T], U8, "key_scale_pool")
-        nc.vector.memset(key_scale_pool[:].bitcast(I32), 0)
+        nc.gpsimd.memset(key_scale_pool[:].bitcast(I32), 0)
         for q in range(4):
             rows = slice(32 * q, 32 * q + 4)
             nc.vector.tensor_copy(key_scale_pool[rows, :].bitcast(I32), key_scale_rows[rows, :].bitcast(I32))
@@ -101,11 +101,6 @@ def tile_attend_tab_wideandown_put_pl_kernel(
 
         identity = tile([P, P], F32, "identity")
         make_identity(nc, identity[:])
-        placed = []
-        for t in range(PACK):
-            window = tile([P, M], F32, f"placed{t}")
-            nc.vector.memset(window[:], 0.0)
-            placed.append(window)
 
         key_words_listed = tile([P, I], U16, "key_words_listed")
         nc.vector.tensor_copy(key_words_listed[:], key_word_pool[:].indirect(token_list[:]))
@@ -121,21 +116,23 @@ def tile_attend_tab_wideandown_put_pl_kernel(
             )
 
         wide = [tile([P, U], F32, f"wide{r}") for r in range(PACK)]
-        for h in range(U // HALF):
-            grouped = tile([P, HALF, PACK], BF16, f"notes_grouped{h}")
-            move(nc, h >= 2, interleaved(grouped[:]), planar(notes_raw[h][:]))
-            codes = tile([P, HALF], U32, f"notes_codes{h}")
-            scales = tile([P, HALF], U8, f"notes_scales{h}")
-            quantise(nc, codes[:], scales[:], grouped[:])
+        for h in range(U // BANK):
+            codes = tile([P, BANK], U32, f"notes_codes{h}")
+            scales = tile([P, BANK], U8, f"notes_scales{h}")
+            for c in range(BANK // HALF):
+                grouped = tile([P, HALF, PACK], BF16, f"notes_grouped{h}{c}")
+                move(nc, 2 * h + c == 3, interleaved(grouped[:]), planar(notes_raw[2 * h + c][:]))
+                cols = slice(c * HALF, (c + 1) * HALF)
+                quantise(nc, codes[:, cols], scales[:, cols], grouped[:])
             for r in range(PACK):
-                bank = bank_tile([P, HALF], r)
+                bank = bank_tile([P, BANK], r)
                 key_product(bank[:], r, codes[:], scales[:])
-                nc.scalar.activation(wide[r][:, h * HALF : (h + 1) * HALF], bank[:], COPY)
+                nc.scalar.activation(wide[r][:, h * BANK : (h + 1) * BANK], bank[:], COPY)
 
         users_listed = tile([P, PACK, J], BF16, "users_listed")
         for t in range(PACK):
             move(nc, True, users_listed[:, t, :], users[t][:].indirect(user_list[:]))
-        users_grouped = tile([P, J, PACK], BF16, "users_grouped")
+        users_grouped = tile([P, J, PACK], BF16, "users_grouped", tag="reused3")
         nc.vector.tensor_copy(interleaved(users_grouped[:]), planar(users_listed[:]))
         users_codes = tile([P, J], U32, "users_codes")
         users_scales = tile([P, J], U8, "users_scales")
@@ -143,8 +140,8 @@ def tile_attend_tab_wideandown_put_pl_kernel(
 
         table = tile([P, PACK, J], F32, "table")
         for r in range(PACK):
-            wide_listed = tile([P, J], F32, f"wide_listed{r}")
-            nc.scalar.activation(wide_listed[:], wide[r][:].indirect(note_list[:]), COPY)
+            wide_listed = tile([P, J], F32, f"wide_listed{r}", tag=f"reused{r}")
+            move(nc, r == 3, wide_listed[:], wide[r][:].indirect(note_list[:]))
             bank = bank_tile([P, J], PACK + r)
             key_product(bank[:], r, users_codes[:], users_scales[:])
             nc.vector.tensor_tensor(table[:, r, :], bank[:], wide_listed[:], ALU.max)
@@ -155,38 +152,55 @@ def tile_attend_tab_wideandown_put_pl_kernel(
         table_scales = tile([P, J], U8, "table_scales")
         quantise(nc, table_codes[:], table_scales[:], table_grouped[:])
 
+        placed = []
+        for t in range(PACK):
+            window = tile([P, M], F32, f"placed{t}", tag=f"reused{t}")
+            nc.gpsimd.memset(window[:], 0.0)
+            placed.append(window)
+
         value_codes = []
         value_scales = []
-        for t in range(PACK):
-            listed = tile([P, I], BF16, f"values_listed{t}")
-            nc.scalar.activation(listed[:], values[t][:].indirect(token_list[:]), COPY)
-            pairs = listed[:].bitcast(F32)
-            bank = bank_tile([P, 2, P], t % 2)
-            for u in range(2):
-                nc.tensor.transpose(bank[:, u, :], pairs[:, u : I // 2 : 2], identity[:])
-            grouped = tile([P, P, PACK], BF16, f"values_grouped{t}")
-            nc.scalar.copy(grouped[:].bitcast(F32), bank[:].rearrange("s u p -> s p u"))
-            codes = tile([P, P], U32, f"values_codes{t}")
-            scales = tile([P, P], U8, f"values_scales{t}")
+        for pair in range(2):
+            bank = bank_tile([P, 2, 2, P], pair)
+            for half in range(2):
+                t = 2 * pair + half
+                listed = tile([P, I], BF16, f"values_listed{t}")
+                nc.scalar.activation(listed[:], values[t][:].indirect(token_list[:]), COPY)
+                pairs = listed[:].bitcast(F32)
+                for u in range(2):
+                    nc.tensor.transpose(bank[:, half, u, :], pairs[:, u : I // 2 : 2], identity[:])
+            grouped = tile([P, 2 * P, PACK], BF16, f"values_grouped{pair}")
+            words = grouped[:].bitcast(F32).rearrange("s (h p) u -> s h p u", h=2)
+            nc.vector.tensor_copy(words, bank[:].rearrange("s h u p -> s h p u"))
+            codes = tile([P, 2 * P], U32, f"values_codes{pair}")
+            scales = tile([P, 2 * P], U8, f"values_scales{pair}")
             quantise(nc, codes[:], scales[:], grouped[:])
-            value_codes.append(codes)
-            value_scales.append(scales)
+            for half in range(2):
+                value_codes.append(codes[:, half * P : (half + 1) * P])
+                value_scales.append(scales[:, half * P : (half + 1) * P])
 
         for t in range(PACK):
-            bank = bank_tile([P, J], (2, 1, 1, 3)[t])
+            bank = bank_tile([P, J], (2, 3, 4, 5)[t])
             nc.tensor.matmul_mx(
-                out=bank[:], lhsT=value_codes[t][:].bitcast(FP8X4), lhsT_scale=value_scales[t][:],
+                out=bank[:], lhsT=value_codes[t].bitcast(FP8X4), lhsT_scale=value_scales[t],
                 rhs=table_codes[:].bitcast(FP8X4), rhs_scale=table_scales[:], start=True, stop=True,
             )
-            product = tile([P, J], F32, f"product{t}")
-            move(nc, t in (0, 3), product[:], bank[:])
-            cuts = ((0, J), (0, HALF, J), (0, HALF, J), (0, SPLIT, J))[t]
-            for a, b in zip(cuts, cuts[1:]):
-                on_vector = t == 0 or (t == 3 and a == 0)
-                part = place_list[:, a // PER_COLUMN : b // PER_COLUMN]
-                move(nc, on_vector, placed[t][:].indirect(part), product[:, a:b])
+            if t == 0:
+                parts = [(0, J, True)]
+            elif t < 3:
+                parts = [(0, J, False)]
+            else:
+                parts = [(0, SPLIT, True), (SPLIT, J, False)]
+            for a, b, on_vector in parts:
+                tag = ("values_listed3", "values3", "product2", "product2" if a > 0 else "")[t]
+                product = tile([P, b - a], F32, f"product{t}_{a}", tag=tag)
+                move(nc, on_vector, product[:], bank[:, a:b])
+                step = HALF if t in (1, 2) else b - a
+                for c in range(a, b, step):
+                    part = place_list[:, c // PER_COLUMN : (c + step) // PER_COLUMN]
+                    move(nc, on_vector, placed[t][:].indirect(part), product[:, c - a : c - a + step])
 
-        result_grouped = [tile([P, BANK, PACK], BF16, f"result_grouped{h}") for h in range(M // BANK)]
+        result_grouped = [tile([P, BANK, PACK], BF16, f"result_grouped{h}", tag="product2" if h else "") for h in range(M // BANK)]
         out_planes = out_0.rearrange("(p t) m -> t p m", t=PACK)
         for pair in range(2):
             result = tile([P, 2, M], F32, f"result{pair}")

@@ -22,7 +22,7 @@ PACK = 4
 BANK = 512
 PER_COLUMN = 16
 HALF = 256
-SPLIT = 128
+SPLIT = 384
 
 
 def interleaved(tile3):
@@ -91,7 +91,7 @@ def tile_attend_tab_wideandown_put_pl_kernel(
         before = [load_plane(old, t, f"before{t}") for t in range(PACK)]
 
         key_scale_pool = tile([P, T], U8, "key_scale_pool")
-        nc.gpsimd.memset(key_scale_pool[:].bitcast(I32), 0)
+        nc.vector.memset(key_scale_pool[:].bitcast(I32), 0)
         for q in range(4):
             rows = slice(32 * q, 32 * q + 4)
             nc.vector.tensor_copy(key_scale_pool[rows, :].bitcast(I32), key_scale_rows[rows, :].bitcast(I32))
@@ -121,15 +121,15 @@ def tile_attend_tab_wideandown_put_pl_kernel(
             scales = tile([P, BANK], U8, f"notes_scales{h}")
             for c in range(BANK // HALF):
                 grouped = tile([P, HALF, PACK], BF16, f"notes_grouped{h}{c}")
-                move(nc, 2 * h + c == 3, interleaved(grouped[:]), planar(notes_raw[2 * h + c][:]))
+                nc.scalar.activation(interleaved(grouped[:]), planar(notes_raw[2 * h + c][:]), COPY)
                 cols = slice(c * HALF, (c + 1) * HALF)
                 quantise(nc, codes[:, cols], scales[:, cols], grouped[:])
             for r in range(PACK):
                 bank = bank_tile([P, BANK], r)
                 key_product(bank[:], r, codes[:], scales[:])
-                nc.scalar.activation(wide[r][:, h * BANK : (h + 1) * BANK], bank[:], COPY)
+                nc.scalar.copy(wide[r][:, h * BANK : (h + 1) * BANK], bank[:])
 
-        users_listed = tile([P, PACK, J], BF16, "users_listed")
+        users_listed = tile([P, PACK, J], F32, "users_listed", tag="reused2")
         for t in range(PACK):
             move(nc, True, users_listed[:, t, :], users[t][:].indirect(user_list[:]))
         users_grouped = tile([P, J, PACK], BF16, "users_grouped", tag="reused3")
@@ -138,24 +138,25 @@ def tile_attend_tab_wideandown_put_pl_kernel(
         users_scales = tile([P, J], U8, "users_scales")
         quantise(nc, users_codes[:], users_scales[:], users_grouped[:])
 
-        table = tile([P, PACK, J], F32, "table")
+        table = tile([P, PACK, J], BF16, "table")
         for r in range(PACK):
             wide_listed = tile([P, J], F32, f"wide_listed{r}", tag=f"reused{r}")
-            move(nc, r == 3, wide_listed[:], wide[r][:].indirect(note_list[:]))
+            move(nc, r >= 2, wide_listed[:], wide[r][:].indirect(note_list[:]))
             bank = bank_tile([P, J], PACK + r)
             key_product(bank[:], r, users_codes[:], users_scales[:])
-            nc.vector.tensor_tensor(table[:, r, :], bank[:], wide_listed[:], ALU.max)
+            larger = tile([P, J], F32, f"larger{r}")
+            nc.vector.tensor_tensor(larger[:], bank[:], wide_listed[:], ALU.max)
+            nc.vector.tensor_scalar(table[:, r, :], larger[:], row_factor[:, r : r + 1], None, ALU.mult)
         table_grouped = tile([P, J, PACK], BF16, "table_grouped")
-        factor = row_factor[:].rearrange("p (a r b) -> p a r b", a=1, b=1).to_broadcast([P, J // 4, PACK, 4])
-        nc.vector.tensor_tensor(interleaved(table_grouped[:]), planar(table[:]), factor, ALU.mult)
+        nc.vector.tensor_copy(interleaved(table_grouped[:]), planar(table[:]))
         table_codes = tile([P, J], U32, "table_codes")
         table_scales = tile([P, J], U8, "table_scales")
         quantise(nc, table_codes[:], table_scales[:], table_grouped[:])
 
         placed = []
         for t in range(PACK):
-            window = tile([P, M], F32, f"placed{t}", tag=f"reused{t}")
-            nc.gpsimd.memset(window[:], 0.0)
+            window = tile([P, M], F32, f"placed{t}", tag="table_grouped" if t == 3 else "")
+            nc.vector.memset(window[:], 0.0)
             placed.append(window)
 
         value_codes = []
@@ -169,9 +170,9 @@ def tile_attend_tab_wideandown_put_pl_kernel(
                 pairs = listed[:].bitcast(F32)
                 for u in range(2):
                     nc.tensor.transpose(bank[:, half, u, :], pairs[:, u : I // 2 : 2], identity[:])
-            grouped = tile([P, 2 * P, PACK], BF16, f"values_grouped{pair}")
+            grouped = tile([P, 2 * P, PACK], BF16, f"values_grouped{pair}", tag="values3" if pair == 0 else "")
             words = grouped[:].bitcast(F32).rearrange("s (h p) u -> s h p u", h=2)
-            nc.vector.tensor_copy(words, bank[:].rearrange("s h u p -> s h p u"))
+            nc.scalar.copy(words, bank[:].rearrange("s h u p -> s h p u"))
             codes = tile([P, 2 * P], U32, f"values_codes{pair}")
             scales = tile([P, 2 * P], U8, f"values_scales{pair}")
             quantise(nc, codes[:], scales[:], grouped[:])
@@ -192,31 +193,36 @@ def tile_attend_tab_wideandown_put_pl_kernel(
             else:
                 parts = [(0, SPLIT, True), (SPLIT, J, False)]
             for a, b, on_vector in parts:
-                tag = ("values_listed3", "values3", "product2", "product2" if a > 0 else "")[t]
+                tag = "product2" if t == 2 or a > 0 else ""
                 product = tile([P, b - a], F32, f"product{t}_{a}", tag=tag)
-                move(nc, on_vector, product[:], bank[:, a:b])
+                if on_vector:
+                    nc.vector.tensor_copy(product[:], bank[:, a:b])
+                else:
+                    nc.scalar.copy(product[:], bank[:, a:b])
                 step = HALF if t in (1, 2) else b - a
                 for c in range(a, b, step):
                     part = place_list[:, c // PER_COLUMN : (c + step) // PER_COLUMN]
                     move(nc, on_vector, placed[t][:].indirect(part), product[:, c - a : c - a + step])
 
-        result_grouped = [tile([P, BANK, PACK], BF16, f"result_grouped{h}", tag="product2" if h else "") for h in range(M // BANK)]
         out_planes = out_0.rearrange("(p t) m -> t p m", t=PACK)
-        for pair in range(2):
-            result = tile([P, 2, M], F32, f"result{pair}")
-            for half in range(2):
-                t = 2 * pair + half
-                nc.vector.tensor_tensor(result[:, half, :], before[t][:], placed[t][:], ALU.add)
-                nc.sync.dma_start(out_planes[t], result[:, half, :])
-            for h in range(M // BANK):
-                cols = slice(h * BANK, (h + 1) * BANK)
-                move(nc, h == 0, interleaved(result_grouped[h][:, :, 2 * pair : 2 * pair + 2]), planar(result[:, :, cols]))
+        result = tile([P, PACK, M], F32, "result")
+        for t in range(PACK):
+            step = BANK if t == 3 else M
+            for a in range(0, M, step):
+                cols = slice(a, a + step)
+                nc.vector.tensor_tensor(result[:, t, cols], before[t][:, cols], placed[t][:, cols], ALU.add)
+            nc.sync.dma_start(out_planes[t], result[:, t, :])
         result_codes = tile([P, M], U32, "result_codes")
         result_scales = tile([P, M], U8, "result_scales")
         words_out = out_1[0].rearrange("p m t -> p (m t)").bitcast(I32)
-        for h in range(M // BANK):
+        for h in reversed(range(M // BANK)):
             cols = slice(h * BANK, (h + 1) * BANK)
-            quantise(nc, result_codes[:, cols], result_scales[:, cols], result_grouped[h][:])
+            grouped = tile([P, BANK, PACK], BF16, f"result_grouped{h}")
+            if h == 1:
+                nc.vector.tensor_copy(interleaved(grouped[:]), planar(result[:, :, cols]))
+            else:
+                nc.scalar.copy(interleaved(grouped[:]), planar(result[:, :, cols]))
+            quantise(nc, result_codes[:, cols], result_scales[:, cols], grouped[:])
             nc.sync.dma_start(words_out[:, cols], result_codes[:, cols].bitcast(I32))
         for q in range(4):
             nc.scalar.dma_start(

from contextlib import ExitStack

import concourse.mybir as mybir
from concourse.masks import make_identity

D, T, I, J, U, Z, E, M = 512, 2048, 512, 512, 1024, 1024, 512, 1024
FLOPS = 2 * D * I * U + 2 * D * I * J + 2 * I * E * J

F32 = mybir.dt.float32
BF16 = mybir.dt.bfloat16
I32 = mybir.dt.int32
U32 = mybir.dt.uint32
U16 = mybir.dt.uint16
U8 = mybir.dt.uint8
FP8X4 = mybir.dt.float8_e4m3fn_x4
FP4X4 = mybir.dt.float4_e2m1fn_x4
COPY = mybir.ActivationFunctionType.Copy
ALU = mybir.AluOpType

P = 128
PACK = 4
BANK = 512
PER_COLUMN = 16
HALF = 256
SPLIT = 384


def interleaved(tile3):
    return tile3.rearrange("p (c x) t -> p c t x", x=4)


def planar(tile3):
    return tile3.rearrange("p t (c x) -> p c t x", x=4)


def quantise(nc, codes, scales, grouped):
    nc.vector.quantize_mx(out=codes.bitcast(FP8X4), scales=scales, in_=grouped.rearrange("p n t -> p (n t)"))


def move(nc, on_vector, out, in_):
    if on_vector:
        nc.vector.tensor_copy(out, in_)
    else:
        nc.scalar.activation(out, in_, COPY)


def tile_attend_tab_wideandown_put_pl_kernel(
    tc, keys_words, keys_scales, notes, users2, rowf, vals, old, offs, offs2, offs3, offs4, out_0, out_1, out_2
):
    nc = tc.nc
    with ExitStack() as ctx:
        sb = ctx.enter_context(tc.tile_pool(name="sb", bufs=1))
        ps = ctx.enter_context(tc.psum_pool(name="ps", bufs=1))

        def tile(shape, dtype, name, tag=""):
            return sb.tile(shape, dtype, name=name, tag=tag, align_bytes=64)

        def load_list(source, name):
            held = sb.tile([P, I // PER_COLUMN], U16, name=name)
            nc.sync.dma_start(held[:], source)
            return held

        def load_plane(source, t, name):
            width = source.shape[1]
            held = tile([P, width], F32, name)
            nc.sync.dma_start(held[:], source.rearrange("(p t) n -> t p n", t=PACK)[t])
            return held

        token_list = load_list(offs, "token_list")
        key_scale_rows = tile([P, T], U8, "key_scale_rows")
        for q in range(4):
            nc.scalar.dma_start(
                key_scale_rows[32 * q : 32 * q + 4, :].bitcast(I32),
                keys_scales[0, 4 * q : 4 * q + 4, :].bitcast(I32),
            )
        key_word_pool = tile([P, T], U16, "key_word_pool")
        nc.sync.dma_start(key_word_pool[:].bitcast(I32), keys_words[0].bitcast(I32))
        notes_by_place = notes.rearrange("(p t) u -> p t u", t=PACK)
        notes_raw = []
        for h in range(U // HALF):
            raw = tile([P, PACK, HALF], F32, f"notes_raw{h}")
            nc.sync.dma_start(raw[:], notes_by_place[:, :, h * HALF : (h + 1) * HALF])
            notes_raw.append(raw)
        user_list = load_list(offs3, "user_list")
        users = [load_plane(users2, t, f"users{t}") for t in range(PACK)]
        note_list = load_list(offs2, "note_list")
        row_factor = tile([P, PACK], F32, "row_factor")
        nc.sync.dma_start(row_factor[:], rowf.rearrange("(s r) one -> s (r one)", r=PACK))
        place_list = load_list(offs4, "place_list")
        values = [load_plane(vals, t, f"values{t}") for t in range(PACK)]
        before = [load_plane(old, t, f"before{t}") for t in range(PACK)]

        key_scale_pool = tile([P, T], U8, "key_scale_pool")
        nc.vector.memset(key_scale_pool[:].bitcast(I32), 0)
        for q in range(4):
            rows = slice(32 * q, 32 * q + 4)
            nc.vector.tensor_copy(key_scale_pool[rows, :].bitcast(I32), key_scale_rows[rows, :].bitcast(I32))

        def bank_tile(shape, number):
            return ps.tile(shape, F32, name=f"bank{number}")

        identity = tile([P, P], F32, "identity")
        make_identity(nc, identity[:])

        key_words_listed = tile([P, I], U16, "key_words_listed")
        nc.vector.tensor_copy(key_words_listed[:], key_word_pool[:].indirect(token_list[:]))
        key_words = tile([P, PACK, P], U16, "key_words")
        nc.vector.tensor_copy(key_words[:], key_words_listed[:].rearrange("p (s r) -> p r s", r=PACK))
        key_scales = tile([P, PACK, P], U8, "key_scales")
        nc.vector.tensor_copy(key_scales[:].rearrange("p r s -> p s r"), key_scale_pool[:].indirect(token_list[:]))

        def key_product(bank, r, codes, scales):
            nc.tensor.matmul_mx(
                out=bank, lhsT=key_words[:, r, :].bitcast(FP4X4), lhsT_scale=key_scales[:, r, :],
                rhs=codes.bitcast(FP8X4), rhs_scale=scales, start=True, stop=True,
            )

        wide = [tile([P, U], F32, f"wide{r}") for r in range(PACK)]
        for h in range(U // BANK):
            codes = tile([P, BANK], U32, f"notes_codes{h}")
            scales = tile([P, BANK], U8, f"notes_scales{h}")
            for c in range(BANK // HALF):
                grouped = tile([P, HALF, PACK], BF16, f"notes_grouped{h}{c}")
                nc.scalar.activation(interleaved(grouped[:]), planar(notes_raw[2 * h + c][:]), COPY)
                cols = slice(c * HALF, (c + 1) * HALF)
                quantise(nc, codes[:, cols], scales[:, cols], grouped[:])
            for r in range(PACK):
                bank = bank_tile([P, BANK], r)
                key_product(bank[:], r, codes[:], scales[:])
                nc.scalar.copy(wide[r][:, h * BANK : (h + 1) * BANK], bank[:])

        users_listed = tile([P, PACK, J], F32, "users_listed", tag="reused2")
        for t in range(PACK):
            move(nc, True, users_listed[:, t, :], users[t][:].indirect(user_list[:]))
        users_grouped = tile([P, J, PACK], BF16, "users_grouped", tag="reused3")
        nc.vector.tensor_copy(interleaved(users_grouped[:]), planar(users_listed[:]))
        users_codes = tile([P, J], U32, "users_codes")
        users_scales = tile([P, J], U8, "users_scales")
        quantise(nc, users_codes[:], users_scales[:], users_grouped[:])

        table = tile([P, PACK, J], BF16, "table")
        for r in range(PACK):
            wide_listed = tile([P, J], F32, f"wide_listed{r}", tag=f"reused{r}")
            move(nc, r >= 2, wide_listed[:], wide[r][:].indirect(note_list[:]))
            bank = bank_tile([P, J], PACK + r)
            key_product(bank[:], r, users_codes[:], users_scales[:])
            larger = tile([P, J], F32, f"larger{r}")
            nc.vector.tensor_tensor(larger[:], bank[:], wide_listed[:], ALU.max)
            nc.vector.tensor_scalar(table[:, r, :], larger[:], row_factor[:, r : r + 1], None, ALU.mult)
        table_grouped = tile([P, J, PACK], BF16, "table_grouped")
        nc.vector.tensor_copy(interleaved(table_grouped[:]), planar(table[:]))
        table_codes = tile([P, J], U32, "table_codes")
        table_scales = tile([P, J], U8, "table_scales")
        quantise(nc, table_codes[:], table_scales[:], table_grouped[:])

        placed = []
        for t in range(PACK):
            window = tile([P, M], F32, f"placed{t}", tag="table_grouped" if t == 3 else "")
            nc.vector.memset(window[:], 0.0)
            placed.append(window)

        value_codes = []
        value_scales = []
        for pair in range(2):
            bank = bank_tile([P, 2, 2, P], pair)
            for half in range(2):
                t = 2 * pair + half
                listed = tile([P, I], BF16, f"values_listed{t}")
                nc.scalar.activation(listed[:], values[t][:].indirect(token_list[:]), COPY)
                pairs = listed[:].bitcast(F32)
                for u in range(2):
                    nc.tensor.transpose(bank[:, half, u, :], pairs[:, u : I // 2 : 2], identity[:])
            grouped = tile([P, 2 * P, PACK], BF16, f"values_grouped{pair}", tag="values3" if pair == 0 else "")
            words = grouped[:].bitcast(F32).rearrange("s (h p) u -> s h p u", h=2)
            nc.scalar.copy(words, bank[:].rearrange("s h u p -> s h p u"))
            codes = tile([P, 2 * P], U32, f"values_codes{pair}")
            scales = tile([P, 2 * P], U8, f"values_scales{pair}")
            quantise(nc, codes[:], scales[:], grouped[:])
            for half in range(2):
                value_codes.append(codes[:, half * P : (half + 1) * P])
                value_scales.append(scales[:, half * P : (half + 1) * P])

        for t in range(PACK):
            bank = bank_tile([P, J], (2, 3, 4, 5)[t])
            nc.tensor.matmul_mx(
                out=bank[:], lhsT=value_codes[t].bitcast(FP8X4), lhsT_scale=value_scales[t],
                rhs=table_codes[:].bitcast(FP8X4), rhs_scale=table_scales[:], start=True, stop=True,
            )
            if t == 0:
                parts = [(0, J, True)]
            elif t < 3:
                parts = [(0, J, False)]
            else:
                parts = [(0, SPLIT, True), (SPLIT, J, False)]
            for a, b, on_vector in parts:
                tag = "product2" if t == 2 or a > 0 else ""
                product = tile([P, b - a], F32, f"product{t}_{a}", tag=tag)
                if on_vector:
                    nc.vector.tensor_copy(product[:], bank[:, a:b])
                else:
                    nc.scalar.copy(product[:], bank[:, a:b])
                step = HALF if t in (1, 2) else b - a
                for c in range(a, b, step):
                    part = place_list[:, c // PER_COLUMN : (c + step) // PER_COLUMN]
                    move(nc, on_vector, placed[t][:].indirect(part), product[:, c - a : c - a + step])

        out_planes = out_0.rearrange("(p t) m -> t p m", t=PACK)
        result = tile([P, PACK, M], F32, "result")
        for t in range(PACK):
            step = BANK if t == 3 else M
            for a in range(0, M, step):
                cols = slice(a, a + step)
                nc.vector.tensor_tensor(result[:, t, cols], before[t][:, cols], placed[t][:, cols], ALU.add)
            nc.sync.dma_start(out_planes[t], result[:, t, :])
        result_codes = tile([P, M], U32, "result_codes")
        result_scales = tile([P, M], U8, "result_scales")
        words_out = out_1[0].rearrange("p m t -> p (m t)").bitcast(I32)
        for h in reversed(range(M // BANK)):
            cols = slice(h * BANK, (h + 1) * BANK)
            grouped = tile([P, BANK, PACK], BF16, f"result_grouped{h}")
            if h == 1:
                nc.vector.tensor_copy(interleaved(grouped[:]), planar(result[:, :, cols]))
            else:
                nc.scalar.copy(interleaved(grouped[:]), planar(result[:, :, cols]))
            quantise(nc, result_codes[:, cols], result_scales[:, cols], grouped[:])
            nc.sync.dma_start(words_out[:, cols], result_codes[:, cols].bitcast(I32))
        for q in range(4):
            nc.scalar.dma_start(
                out_2[0, 4 * q : 4 * q + 4, :].bitcast(I32), result_scales[32 * q : 32 * q + 4, :].bitcast(I32)
            )
